import numpy as np
import ml_dtypes


def mxq(x, axis, fmt="e4m3"):
    dtype, down = {"e4m3": (ml_dtypes.float8_e4m3fn, 7), "e5m2": (ml_dtypes.float8_e5m2, 14)}[fmt]
    v = np.moveaxis(np.asarray(x, np.float32).astype(ml_dtypes.bfloat16).astype(np.float64), axis, -1)
    blocks = v.reshape(v.shape[:-1] + (-1, 32))
    amax = np.abs(blocks).max(-1, keepdims=True)
    byte = np.maximum(np.where(amax > 0, np.frexp(amax)[1] - 1 + 127, 0) - down, 1)
    scale = np.exp2(byte - 127.0)
    codes = (blocks / scale).astype(np.float32).astype(dtype).astype(np.float64)
    return np.moveaxis((codes * scale).reshape(v.shape), -1, axis)


WIDE = False


def mx_kscale(k):
    if not WIDE:
        return np.ones(k)
    levels = np.array([10, -10, 5, -5, 0])
    if k % 512:
        return np.exp2(np.random.permutation(np.resize(levels, k // 32))).repeat(32)
    a = np.empty((k // 512, 16))
    for p in range(k // 512):
        a[p, :8] = np.random.permutation(np.resize(levels, 8))
        for g in range(8):
            far = levels[np.abs(levels - a[p, g]) >= 10]
            a[p, g + 8] = far[np.random.randint(len(far))]
    return np.exp2(a.ravel()).repeat(32)


def f64(x):
    return np.asarray(x).astype(np.float64)


def striped(idx):
    return np.tile(idx.reshape(-1, 16).T, (8, 1)).astype(np.uint16)


def unstriped(offs):
    return offs[:16].T.reshape(-1).astype(np.int64)


def silu(v):
    return v / (1.0 + np.exp(-np.maximum(v, -700.0)))


K, T, S, H, N = 512, 2048, 1024, 1024, 512


def setup_inputs():
    n = np.random.standard_normal
    s = mx_kscale(K)[:, None]
    u = mx_kscale(H)
    return {
        "xT": (n((K, T)) * s).astype(np.float32),
        "w1": (n((K, H)) / np.sqrt(K) / s).astype(np.float32),
        "w3": (n((K, H)) / np.sqrt(K) / s * u).astype(np.float32),
        "w2": (n((H, N)) / np.sqrt(H) / u[:, None]).astype(np.float32),
        "offs": striped(np.sort(np.random.permutation(T)[:S])),
    }


def reference(xT, w1, w3, w2, offs):
    idx = unstriped(offs)
    xq = mxq(f64(xT)[:, idx], 0, "e4m3")
    h = silu(mxq(f64(w1), 0, "e4m3").T @ xq) * (mxq(f64(w3), 0, "e4m3").T @ xq)
    y = mxq(f64(w2), 0, "e4m3").T @ mxq(h, 0, "e4m3")
    return y

@@ -1,0 +1,242 @@
+from contextlib import ExitStack
+
+import concourse.mybir as mybir
+
+K, T, S, H, N = 512, 2048, 1024, 1024, 512
+
+F32 = mybir.dt.float32
+BF16 = mybir.dt.bfloat16
+U32 = mybir.dt.uint32
+U16 = mybir.dt.uint16
+U8 = mybir.dt.uint8
+FP8X4 = mybir.dt.float8_e4m3fn_x4
+COPY = mybir.ActivationFunctionType.Copy
+SILU = mybir.ActivationFunctionType.Silu
+MULT = mybir.AluOpType.mult
+
+P = 128
+PACK = 4
+PASS = P * PACK
+HALF = 512
+SLICE = 128
+FLOPS = 2 * S * (2 * K * H + H * N)
+
+
+def tile_picked_pick_glu_silu_srt_e_kernel(tc, xT, w1, w3, w2, offs, out):
+    nc = tc.nc
+    with ExitStack() as ctx:
+        keep = ctx.enter_context(tc.tile_pool(name="keep", bufs=1))
+        ring = ctx.enter_context(tc.tile_pool(name="ring", bufs=4))
+        acc = ctx.enter_context(tc.psum_pool(name="acc", bufs=4))
+
+        offsets = keep.tile([P, S // 16], U16, name="offsets")
+
+        def load(name, source):
+            raw = keep.tile([P, PACK, 512], F32, name=name, align_bytes=64)
+            nc.sync.dma_start(out=raw[:], in_=source.rearrange("(p j) c -> p j c", j=PACK))
+            return raw
+
+        warm = keep.tile([P, 1], F32, name="warm")
+        nc.vector.memset(warm[:], 0.0)
+        nc.scalar.activation(warm[:], warm[:], SILU)
+        all_bytes = keep.tile([P, T], U8, name="all_bytes", align_bytes=64)
+        nc.gpsimd.memset(all_bytes[:], 0)
+        all_words = keep.tile([P, T], U32, name="all_words", align_bytes=64)
+
+        x_raw = [None] * 4
+        x_raw[0] = load("x_raw0", xT[:, 0:512])
+        nc.sync.dma_start(offsets[:], offs)
+        x_raw[1] = load("x_raw1", xT[:, 512:1024])
+        x_raw[2] = load("x_raw2", xT[:, 1024:1536])
+        w_raw = {}
+        w_raw[1, 0] = load("w1_raw0", w1[:, 0:512])
+        w_raw[3, 0] = load("w3_raw0", w3[:, 0:512])
+        x_raw[3] = load("x_raw3", xT[:, 1536:2048])
+        w_raw[1, 1] = load("w1_raw1", w1[:, 512:1024])
+        w_raw[3, 1] = load("w3_raw1", w3[:, 512:1024])
+        w_raw[2, 0] = load("w2_raw0", w2[0:512, :])
+        w_raw[2, 1] = load("w2_raw1", w2[512:1024, :])
+
+        def cast(name, dst_view, src_view, on_vector, count):
+            if on_vector:
+                nc.vector.tensor_copy(out=dst_view[:, 0:on_vector], in_=src_view[:, 0:on_vector])
+            if on_vector < count:
+                nc.scalar.activation(dst_view[:, on_vector:count], src_view[:, on_vector:count], COPY)
+
+        x_grouped = {}
+        w_grouped = {}
+        w_codes = {}
+        w_scales = {}
+
+        def cast_x(c, on_vector):
+            grouped = keep.tile([P, 512, PACK], BF16, name="x_grouped%d" % c, align_bytes=64)
+            cast("x", grouped[:], x_raw[c][:].rearrange("p j c -> p c j"), on_vector, 512)
+            x_grouped[c] = grouped
+
+        def quantize_x(c):
+            cols = slice(c * 512, (c + 1) * 512)
+            nc.vector.quantize_mx(
+                out=all_words[:, cols].bitcast(FP8X4),
+                scales=all_bytes[:, cols],
+                in_=x_grouped[c][:].rearrange("p c j -> p (c j)"),
+            )
+
+        def cast_w(layer, g, on_vector):
+            grouped = keep.tile([P, 2048], BF16, name="w%d_grouped%d" % (layer, g), align_bytes=64)
+            raw = w_raw[layer, g]
+            if layer == 2:
+                dst = grouped[:].rearrange("p (c j) -> p c j", j=PACK)
+                src = raw[:].rearrange("p j c -> p c j")
+                for c0 in (0, 256):
+                    part = slice(c0, c0 + 256)
+                    nc.gpsimd.tensor_scalar(
+                        out=dst[:, part], in0=src[:, part], scalar1=1.0, scalar2=0.0, op0=MULT, op1=mybir.AluOpType.add
+                    )
+            else:
+                cast(
+                    "w",
+                    grouped[:].rearrange("p (t m j) -> p m t j", t=PACK, j=PACK),
+                    raw[:].rearrange("p j (m t) -> p m t j", t=PACK),
+                    on_vector,
+                    128,
+                )
+            w_grouped[layer, g] = grouped
+
+        def quantize_w(layer, g):
+            codes = keep.tile([P, 512], U32, name="w%d_codes%d" % (layer, g), align_bytes=64)
+            scales = keep.tile([P, 512], U8, name="w%d_scales%d" % (layer, g), align_bytes=64)
+            nc.vector.quantize_mx(out=codes[:].bitcast(FP8X4), scales=scales[:], in_=w_grouped[layer, g][:])
+            w_codes[layer, g] = codes
+            w_scales[layer, g] = scales
+
+        picked_words = []
+        picked_bytes = []
+        for half in range(2):
+            words = keep.tile([P, HALF], U32, name="picked_words%d" % half, align_bytes=64)
+            scale_bytes = keep.tile([P, HALF], U8, name="picked_bytes%d" % half, align_bytes=64)
+            picked_words.append(words)
+            picked_bytes.append(scale_bytes)
+
+        def gather(half):
+            reach = (half + 1) * HALF + T - S
+            entries = offsets[:, half * HALF // 16 : (half + 1) * HALF // 16]
+            nc.vector.tensor_copy(out=picked_words[half][:], in_=all_words[:, 0:reach].indirect(entries))
+            nc.vector.tensor_copy(out=picked_bytes[half][:], in_=all_bytes[:, 0:reach].indirect(entries))
+
+        h_grouped = {}
+        h_codes = {}
+        h_scales = {}
+
+        def unit(g, half, s):
+            if s == 0:
+                fresh = ring.tile([P, HALF, PACK], BF16, name="h_grouped", align_bytes=64)
+                h_grouped[g, half] = fresh
+            cols = slice(s * SLICE, (s + 1) * SLICE)
+            gate = acc.tile([P, PACK, SLICE], F32, name="gate", tag="gate")
+            up = acc.tile([P, PACK, SLICE], F32, name="up", tag="up")
+            for layer, bank in ((1, gate), (3, up)):
+                for t in range(PACK):
+                    rows = slice(t * P, (t + 1) * P)
+                    nc.tensor.matmul_mx(
+                        out=bank[:, t, :],
+                        lhsT=w_codes[layer, g][:, rows].bitcast(FP8X4),
+                        lhsT_scale=w_scales[layer, g][:, rows],
+                        rhs=picked_words[half][:, cols].bitcast(FP8X4),
+                        rhs_scale=picked_bytes[half][:, cols],
+                        start=True,
+                        stop=True,
+                    )
+            act = ring.tile([P, SLICE, PACK], F32, name="act")
+            nc.scalar.activation(act[:], gate[:].rearrange("p t n -> p n t"), SILU)
+            nc.vector.tensor_tensor(
+                out=h_grouped[g, half][:, cols, :], in0=up[:].rearrange("p t n -> p n t"), in1=act[:], op=MULT
+            )
+
+        def quantize_h(g, half):
+            codes = keep.tile([P, HALF], U32, name="h_codes%d%d" % (g, half), align_bytes=64)
+            scales = keep.tile([P, HALF], U8, name="h_scales%d%d" % (g, half), align_bytes=64)
+            nc.vector.quantize_mx(
+                out=codes[:].bitcast(FP8X4),
+                scales=scales[:],
+                in_=h_grouped[g, half][:].rearrange("p n t -> p (n t)"),
+            )
+            h_codes[g, half] = codes
+            h_scales[g, half] = scales
+
+        y_bank = {}
+
+        def product(half, m, g):
+            if g == 0:
+                bank = acc.tile([P, HALF], F32, name="y%d%d" % (half, m), tag="gate" if m % 2 == 0 else "up")
+                y_bank[half, m] = bank
+            rows = slice(m * P, (m + 1) * P)
+            nc.tensor.matmul_mx(
+                out=y_bank[half, m][:],
+                lhsT=w_codes[2, g][:, rows].bitcast(FP8X4),
+                lhsT_scale=w_scales[2, g][:, rows],
+                rhs=h_codes[g, half][:].bitcast(FP8X4),
+                rhs_scale=h_scales[g, half][:],
+                start=(g == 0),
+                stop=(g == 1),
+            )
+
+        def store(half, m):
+            y = keep.tile([P, HALF], F32, name="y_out%d%d" % (half, m))
+            if m % 2 == 0:
+                nc.scalar.copy(y[:], y_bank[half, m][:])
+            else:
+                nc.vector.tensor_copy(out=y[:], in_=y_bank[half, m][:])
+            nc.sync.dma_start(out=out[m * P : (m + 1) * P, half * HALF : (half + 1) * HALF], in_=y[:])
+
+        for c in range(3):
+            cast_x(c, 320)
+            quantize_x(c)
+        gather(0)
+        cast_w(1, 0, 80)
+        quantize_w(1, 0)
+        cast_w(3, 0, 80)
+        quantize_w(3, 0)
+
+        unit(0, 0, 0)
+        cast_x(3, 192)
+        unit(0, 0, 1)
+        quantize_x(3)
+        gather(1)
+        unit(0, 0, 2)
+        unit(0, 0, 3)
+        cast_w(1, 1, 16)
+        unit(0, 1, 0)
+        quantize_h(0, 0)
+        unit(0, 1, 1)
+        quantize_w(1, 1)
+        cast_w(3, 1, 16)
+        unit(0, 1, 2)
+        unit(0, 1, 3)
+        quantize_w(3, 1)
+        unit(1, 0, 0)
+        quantize_h(0, 1)
+        cast_w(2, 0, 40)
+        unit(1, 0, 1)
+        unit(1, 0, 2)
+        quantize_w(2, 0)
+        unit(1, 0, 3)
+        cast_w(2, 1, 40)
+        unit(1, 1, 0)
+        quantize_h(1, 0)
+        unit(1, 1, 1)
+        quantize_w(2, 1)
+        for m in range(4):
+            product(0, m, 0)
+            product(0, m, 1)
+        unit(1, 1, 2)
+        store(0, 0)
+        store(0, 1)
+        unit(1, 1, 3)
+        store(0, 2)
+        store(0, 3)
+        for m in range(4):
+            product(1, m, 0)
+        quantize_h(1, 1)
+        for m in range(4):
+            product(1, m, 1)
+            store(1, m)

@@ -17,7 +17,6 @@ MULT = mybir.AluOpType.mult
 P = 128
 PACK = 4
 PASS = P * PACK
-HALF = 512
 SLICE = 128
 FLOPS = 2 * S * (2 * K * H + H * N)
 
@@ -30,12 +29,6 @@ def tile_picked_pick_glu_silu_srt_e_kernel(tc, xT, w1, w3, w2, offs, out):
         acc = ctx.enter_context(tc.psum_pool(name="acc", bufs=4))
 
         offsets = keep.tile([P, S // 16], U16, name="offsets")
-
-        def load(name, source):
-            raw = keep.tile([P, PACK, 512], F32, name=name, align_bytes=64)
-            nc.sync.dma_start(out=raw[:], in_=source.rearrange("(p j) c -> p j c", j=PACK))
-            return raw
-
         warm = keep.tile([P, 1], F32, name="warm")
         nc.vector.memset(warm[:], 0.0)
         nc.scalar.activation(warm[:], warm[:], SILU)
@@ -43,200 +36,180 @@ def tile_picked_pick_glu_silu_srt_e_kernel(tc, xT, w1, w3, w2, offs, out):
         nc.gpsimd.memset(all_bytes[:], 0)
         all_words = keep.tile([P, T], U32, name="all_words", align_bytes=64)
 
-        x_raw = [None] * 4
-        x_raw[0] = load("x_raw0", xT[:, 0:512])
-        nc.sync.dma_start(offsets[:], offs)
-        x_raw[1] = load("x_raw1", xT[:, 512:1024])
-        x_raw[2] = load("x_raw2", xT[:, 1024:1536])
-        w_raw = {}
-        w_raw[1, 0] = load("w1_raw0", w1[:, 0:512])
-        w_raw[3, 0] = load("w3_raw0", w3[:, 0:512])
-        x_raw[3] = load("x_raw3", xT[:, 1536:2048])
-        w_raw[1, 1] = load("w1_raw1", w1[:, 512:1024])
-        w_raw[3, 1] = load("w3_raw1", w3[:, 512:1024])
-        w_raw[2, 0] = load("w2_raw0", w2[0:512, :])
-        w_raw[2, 1] = load("w2_raw1", w2[512:1024, :])
+        sources = {}
+        for c in range(4):
+            sources["x%d" % c] = xT[:, c * 512 : (c + 1) * 512]
+        for g in range(2):
+            sources["w1_%d" % g] = w1[:, g * 512 : (g + 1) * 512]
+            sources["w3_%d" % g] = w3[:, g * 512 : (g + 1) * 512]
+            sources["w2_%d" % g] = w2[g * 512 : (g + 1) * 512, :]
+        raw = {}
+        for name in ["x0","offs","x1","x2","x3","w1_0","w3_0","w1_1","w3_1","w2_0","w2_1"]:
+            if name == "offs":
+                nc.sync.dma_start(offsets[:], offs)
+            else:
+                tile = keep.tile([P, PACK, 512], F32, name="raw_" + name, align_bytes=64)
+                nc.sync.dma_start(out=tile[:], in_=sources[name].rearrange("(p j) c -> p j c", j=PACK))
+                raw[name] = tile
 
-        def cast(name, dst_view, src_view, on_vector, count):
-            if on_vector:
-                nc.vector.tensor_copy(out=dst_view[:, 0:on_vector], in_=src_view[:, 0:on_vector])
-            if on_vector < count:
-                nc.scalar.activation(dst_view[:, on_vector:count], src_view[:, on_vector:count], COPY)
+        grouped = {}
+        codes = {}
+        scales = {}
 
-        x_grouped = {}
-        w_grouped = {}
-        w_codes = {}
-        w_scales = {}
-
-        def cast_x(c, on_vector):
-            grouped = keep.tile([P, 512, PACK], BF16, name="x_grouped%d" % c, align_bytes=64)
-            cast("x", grouped[:], x_raw[c][:].rearrange("p j c -> p c j"), on_vector, 512)
-            x_grouped[c] = grouped
-
-        def quantize_x(c):
-            cols = slice(c * 512, (c + 1) * 512)
-            nc.vector.quantize_mx(
-                out=all_words[:, cols].bitcast(FP8X4),
-                scales=all_bytes[:, cols],
-                in_=x_grouped[c][:].rearrange("p c j -> p (c j)"),
-            )
-
-        def cast_w(layer, g, on_vector):
-            grouped = keep.tile([P, 2048], BF16, name="w%d_grouped%d" % (layer, g), align_bytes=64)
-            raw = w_raw[layer, g]
-            if layer == 2:
-                dst = grouped[:].rearrange("p (c j) -> p c j", j=PACK)
-                src = raw[:].rearrange("p j c -> p c j")
-                for c0 in (0, 256):
-                    part = slice(c0, c0 + 256)
+        def cast(name, shares):
+            tile = keep.tile([P, 2048], BF16, name="grouped_" + name, align_bytes=64)
+            grouped[name] = tile
+            if name[:2] in ("w1", "w3"):
+                dst = tile[:].rearrange("p (t m j) -> p m t j", t=PACK, j=PACK)
+                src = raw[name][:].rearrange("p j (m t) -> p m t j", t=PACK)
+                scale = 1
+            else:
+                dst = tile[:].rearrange("p (c j) -> p c j", j=PACK)
+                src = raw[name][:].rearrange("p j c -> p c j")
+                scale = 4
+            start = 0
+            for engine, count in shares:
+                part = slice(start * scale, (start + count) * scale)
+                if engine == "V":
+                    nc.vector.tensor_copy(out=dst[:, part], in_=src[:, part])
+                elif engine == "S":
+                    nc.scalar.activation(dst[:, part], src[:, part], COPY)
+                else:
                     nc.gpsimd.tensor_scalar(
                         out=dst[:, part], in0=src[:, part], scalar1=1.0, scalar2=0.0, op0=MULT, op1=mybir.AluOpType.add
                     )
+                start = start + count
+            assert start == 128
+
+        def quantize(name):
+            if name[0] == "x":
+                cols = slice(int(name[1:]) * 512, (int(name[1:]) + 1) * 512)
+                nc.vector.quantize_mx(out=all_words[:, cols].bitcast(FP8X4), scales=all_bytes[:, cols], in_=grouped[name][:])
             else:
-                cast(
-                    "w",
-                    grouped[:].rearrange("p (t m j) -> p m t j", t=PACK, j=PACK),
-                    raw[:].rearrange("p j (m t) -> p m t j", t=PACK),
-                    on_vector,
-                    128,
-                )
-            w_grouped[layer, g] = grouped
+                code = keep.tile([P, 512], U32, name="codes_" + name, align_bytes=64)
+                scale = keep.tile([P, 512], U8, name="scales_" + name, align_bytes=64)
+                nc.vector.quantize_mx(out=code[:].bitcast(FP8X4), scales=scale[:], in_=grouped[name][:])
+                codes[name] = code
+                scales[name] = scale
 
-        def quantize_w(layer, g):
-            codes = keep.tile([P, 512], U32, name="w%d_codes%d" % (layer, g), align_bytes=64)
-            scales = keep.tile([P, 512], U8, name="w%d_scales%d" % (layer, g), align_bytes=64)
-            nc.vector.quantize_mx(out=codes[:].bitcast(FP8X4), scales=scales[:], in_=w_grouped[layer, g][:])
-            w_codes[layer, g] = codes
-            w_scales[layer, g] = scales
+        picked_words = keep.tile([P, S], U32, name="picked_words", align_bytes=64)
+        picked_bytes = keep.tile([P, S], U8, name="picked_bytes", align_bytes=64)
 
-        picked_words = []
-        picked_bytes = []
-        for half in range(2):
-            words = keep.tile([P, HALF], U32, name="picked_words%d" % half, align_bytes=64)
-            scale_bytes = keep.tile([P, HALF], U8, name="picked_bytes%d" % half, align_bytes=64)
-            picked_words.append(words)
-            picked_bytes.append(scale_bytes)
+        def gather(first, last):
+            reach = last + T - S
+            entries = offsets[:, first // 16 : last // 16]
+            nc.vector.tensor_copy(out=picked_words[:, first:last], in_=all_words[:, 0:reach].indirect(entries))
+            nc.vector.tensor_copy(out=picked_bytes[:, first:last], in_=all_bytes[:, 0:reach].indirect(entries))
 
-        def gather(half):
-            reach = (half + 1) * HALF + T - S
-            entries = offsets[:, half * HALF // 16 : (half + 1) * HALF // 16]
-            nc.vector.tensor_copy(out=picked_words[half][:], in_=all_words[:, 0:reach].indirect(entries))
-            nc.vector.tensor_copy(out=picked_bytes[half][:], in_=all_bytes[:, 0:reach].indirect(entries))
+        h_grouped = []
+        h_codes = []
+        h_scales = []
+        for g in range(2):
+            a = keep.tile([P, S, PACK], BF16, name="h_grouped%d" % g, align_bytes=64)
+            b = keep.tile([P, S], U32, name="h_codes%d" % g, align_bytes=64)
+            c = keep.tile([P, S], U8, name="h_scales%d" % g, align_bytes=64)
+            h_grouped.append(a)
+            h_codes.append(b)
+            h_scales.append(c)
 
-        h_grouped = {}
-        h_codes = {}
-        h_scales = {}
-
-        def unit(g, half, s):
-            if s == 0:
-                fresh = ring.tile([P, HALF, PACK], BF16, name="h_grouped", align_bytes=64)
-                h_grouped[g, half] = fresh
+        def unit(g, s):
             cols = slice(s * SLICE, (s + 1) * SLICE)
             gate = acc.tile([P, PACK, SLICE], F32, name="gate", tag="gate")
             up = acc.tile([P, PACK, SLICE], F32, name="up", tag="up")
-            for layer, bank in ((1, gate), (3, up)):
+            for layer, bank in (("w1_%d", gate), ("w3_%d", up)):
                 for t in range(PACK):
                     rows = slice(t * P, (t + 1) * P)
                     nc.tensor.matmul_mx(
                         out=bank[:, t, :],
-                        lhsT=w_codes[layer, g][:, rows].bitcast(FP8X4),
-                        lhsT_scale=w_scales[layer, g][:, rows],
-                        rhs=picked_words[half][:, cols].bitcast(FP8X4),
-                        rhs_scale=picked_bytes[half][:, cols],
+                        lhsT=codes[layer % g][:, rows].bitcast(FP8X4),
+                        lhsT_scale=scales[layer % g][:, rows],
+                        rhs=picked_words[:, cols].bitcast(FP8X4),
+                        rhs_scale=picked_bytes[:, cols],
                         start=True,
                         stop=True,
                     )
             act = ring.tile([P, SLICE, PACK], F32, name="act")
             nc.scalar.activation(act[:], gate[:].rearrange("p t n -> p n t"), SILU)
-            nc.vector.tensor_tensor(
-                out=h_grouped[g, half][:, cols, :], in0=up[:].rearrange("p t n -> p n t"), in1=act[:], op=MULT
-            )
+            nc.vector.tensor_tensor(out=h_grouped[g][:, cols, :], in0=up[:].rearrange("p t n -> p n t"), in1=act[:], op=MULT)
 
-        def quantize_h(g, half):
-            codes = keep.tile([P, HALF], U32, name="h_codes%d%d" % (g, half), align_bytes=64)
-            scales = keep.tile([P, HALF], U8, name="h_scales%d%d" % (g, half), align_bytes=64)
+        def quantize_h(g, first, last):
             nc.vector.quantize_mx(
-                out=codes[:].bitcast(FP8X4),
-                scales=scales[:],
-                in_=h_grouped[g, half][:].rearrange("p n t -> p (n t)"),
-            )
-            h_codes[g, half] = codes
-            h_scales[g, half] = scales
-
-        y_bank = {}
-
-        def product(half, m, g):
-            if g == 0:
-                bank = acc.tile([P, HALF], F32, name="y%d%d" % (half, m), tag="gate" if m % 2 == 0 else "up")
-                y_bank[half, m] = bank
-            rows = slice(m * P, (m + 1) * P)
-            nc.tensor.matmul_mx(
-                out=y_bank[half, m][:],
-                lhsT=w_codes[2, g][:, rows].bitcast(FP8X4),
-                lhsT_scale=w_scales[2, g][:, rows],
-                rhs=h_codes[g, half][:].bitcast(FP8X4),
-                rhs_scale=h_scales[g, half][:],
-                start=(g == 0),
-                stop=(g == 1),
+                out=h_codes[g][:, first:last].bitcast(FP8X4),
+                scales=h_scales[g][:, first:last],
+                in_=h_grouped[g][:, first:last, :].rearrange("p n t -> p (n t)"),
             )
 
-        def store(half, m):
-            y = keep.tile([P, HALF], F32, name="y_out%d%d" % (half, m))
-            if m % 2 == 0:
-                nc.scalar.copy(y[:], y_bank[half, m][:])
-            else:
-                nc.vector.tensor_copy(out=y[:], in_=y_bank[half, m][:])
-            nc.sync.dma_start(out=out[m * P : (m + 1) * P, half * HALF : (half + 1) * HALF], in_=y[:])
+        def output(first, last, engines):
+            width = last - first
+            per_bank = 512 // width
+            m = 0
+            for number, engine in enumerate(engines):
+                bank = acc.tile([P, per_bank, width], F32, name="y%d_%d" % (first, number), tag="gate" if number % 2 == 0 else "up")
+                for i in range(per_bank):
+                    rows = slice((m + i) * P, (m + i + 1) * P)
+                    for g in range(2):
+                        nc.tensor.matmul_mx(
+                            out=bank[:, i, :],
+                            lhsT=codes["w2_%d" % g][:, rows].bitcast(FP8X4),
+                            lhsT_scale=scales["w2_%d" % g][:, rows],
+                            rhs=h_codes[g][:, first:last].bitcast(FP8X4),
+                            rhs_scale=h_scales[g][:, first:last],
+                            start=(g == 0),
+                            stop=(g == 1),
+                        )
+                y = keep.tile([P, per_bank, width], F32, name="y_out%d_%d" % (first, number))
+                if engine == "S":
+                    nc.scalar.copy(y[:], bank[:])
+                else:
+                    nc.vector.tensor_copy(out=y[:], in_=bank[:])
+                nc.sync.dma_start(
+                    out=out[m * P : (m + per_bank) * P, first:last].rearrange("(i p) n -> p i n", p=P), in_=y[:]
+                )
+                m = m + per_bank
 
-        for c in range(3):
-            cast_x(c, 320)
-            quantize_x(c)
-        gather(0)
-        cast_w(1, 0, 80)
-        quantize_w(1, 0)
-        cast_w(3, 0, 80)
-        quantize_w(3, 0)
-
-        unit(0, 0, 0)
-        cast_x(3, 192)
-        unit(0, 0, 1)
-        quantize_x(3)
-        gather(1)
-        unit(0, 0, 2)
-        unit(0, 0, 3)
-        cast_w(1, 1, 16)
-        unit(0, 1, 0)
-        quantize_h(0, 0)
-        unit(0, 1, 1)
-        quantize_w(1, 1)
-        cast_w(3, 1, 16)
-        unit(0, 1, 2)
-        unit(0, 1, 3)
-        quantize_w(3, 1)
-        unit(1, 0, 0)
-        quantize_h(0, 1)
-        cast_w(2, 0, 40)
-        unit(1, 0, 1)
-        unit(1, 0, 2)
-        quantize_w(2, 0)
-        unit(1, 0, 3)
-        cast_w(2, 1, 40)
-        unit(1, 1, 0)
-        quantize_h(1, 0)
-        unit(1, 1, 1)
-        quantize_w(2, 1)
-        for m in range(4):
-            product(0, m, 0)
-            product(0, m, 1)
-        unit(1, 1, 2)
-        store(0, 0)
-        store(0, 1)
-        unit(1, 1, 3)
-        store(0, 2)
-        store(0, 3)
-        for m in range(4):
-            product(1, m, 0)
-        quantize_h(1, 1)
-        for m in range(4):
-            product(1, m, 1)
-            store(1, m)
+        cast("x0", (("V", 32), ("S", 96)))
+        quantize("x0")
+        cast("x1", (("V", 32), ("S", 96)))
+        quantize("x1")
+        cast("x2", (("V", 32), ("S", 96)))
+        quantize("x2")
+        gather(0, 512)
+        cast("x3", (("V", 32), ("S", 96)))
+        quantize("x3")
+        gather(512, 1024)
+        cast("w1_0", (("S", 128),))
+        quantize("w1_0")
+        cast("w3_0", (("V", 80), ("S", 48)))
+        quantize("w3_0")
+        unit(0, 0)
+        unit(0, 1)
+        cast("w1_1", (("V", 16), ("S", 112)))
+        unit(0, 2)
+        quantize("w1_1")
+        unit(0, 3)
+        cast("w3_1", (("V", 16), ("S", 112)))
+        unit(0, 4)
+        quantize_h(0, 0, 512)
+        quantize("w3_1")
+        unit(1, 0)
+        unit(1, 1)
+        cast("w2_0", (("V", 16), ("S", 112)))
+        unit(1, 2)
+        quantize("w2_0")
+        unit(1, 3)
+        cast("w2_1", (("V", 16), ("S", 112)))
+        unit(0, 5)
+        quantize_h(1, 0, 512)
+        unit(0, 6)
+        quantize("w2_1")
+        output(0, 512, "SVSV")
+        unit(0, 7)
+        unit(1, 4)
+        quantize_h(0, 512, 1024)
+        unit(1, 5)
+        unit(1, 6)
+        quantize_h(1, 512, 768)
+        unit(1, 7)
+        output(512, 768, "SV")
+        quantize_h(1, 768, 1024)
+        output(768, 1024, "SV")

@@ -60,16 +60,14 @@ def tile_picked_pick_glu_silu_srt_e_kernel(tc, xT, w1, w3, w2, offs, out):
             tile = keep.tile([P, 2048], BF16, name="grouped_" + name, align_bytes=64)
             grouped[name] = tile
             if name[:2] in ("w1", "w3"):
-                dst = tile[:].rearrange("p (t m j) -> p m t j", t=PACK, j=PACK)
-                src = raw[name][:].rearrange("p j (m t) -> p m t j", t=PACK)
-                scale = 1
+                dst = tile[:].rearrange("p (t m j) -> p m j t", t=PACK, j=PACK)
+                src = raw[name][:].rearrange("p j (m t) -> p m j t", t=PACK)
             else:
-                dst = tile[:].rearrange("p (c j) -> p c j", j=PACK)
-                src = raw[name][:].rearrange("p j c -> p c j")
-                scale = 4
+                dst = tile[:].rearrange("p (c i j) -> p c j i", i=4, j=PACK)
+                src = raw[name][:].rearrange("p j (c i) -> p c j i", i=4)
             start = 0
             for engine, count in shares:
-                part = slice(start * scale, (start + count) * scale)
+                part = slice(start, start + count)
                 if engine == "V":
                     nc.vector.tensor_copy(out=dst[:, part], in_=src[:, part])
                 elif engine == "S":

@@ -49,7 +49,12 @@ def tile_picked_pick_glu_silu_srt_e_kernel(tc, xT, w1, w3, w2, offs, out):
                 nc.sync.dma_start(offsets[:], offs)
             else:
                 tile = keep.tile([P, PACK, 512], F32, name="raw_" + name, align_bytes=64)
-                nc.sync.dma_start(out=tile[:], in_=sources[name].rearrange("(p j) c -> p j c", j=PACK))
+                source = sources[name].rearrange("(p j) c -> p j c", j=PACK)
+                if name == "x0":
+                    for part in (slice(0, 256), slice(256, 512)):
+                        nc.sync.dma_start(out=tile[:, :, part], in_=source[:, :, part])
+                else:
+                    nc.sync.dma_start(out=tile[:], in_=source)
                 raw[name] = tile
 
         grouped = {}
@@ -73,8 +78,14 @@ def tile_picked_pick_glu_silu_srt_e_kernel(tc, xT, w1, w3, w2, offs, out):
                 elif engine == "S":
                     nc.scalar.activation(dst[:, part], src[:, part], COPY)
                 else:
+                    cols = slice(start * 4, (start + count) * 4)
                     nc.gpsimd.tensor_scalar(
-                        out=dst[:, part], in0=src[:, part], scalar1=1.0, scalar2=0.0, op0=MULT, op1=mybir.AluOpType.add
+                        out=tile[:].rearrange("p (c j) -> p c j", j=PACK)[:, cols],
+                        in0=raw[name][:].rearrange("p j c -> p c j")[:, cols],
+                        scalar1=1.0,
+                        scalar2=0.0,
+                        op0=MULT,
+                        op1=mybir.AluOpType.add,
                     )
                 start = start + count
             assert start == 128
@@ -93,11 +104,10 @@ def tile_picked_pick_glu_silu_srt_e_kernel(tc, xT, w1, w3, w2, offs, out):
         picked_words = keep.tile([P, S], U32, name="picked_words", align_bytes=64)
         picked_bytes = keep.tile([P, S], U8, name="picked_bytes", align_bytes=64)
 
-        def gather(first, last):
+        def gather(picked, window, first, last):
             reach = last + T - S
             entries = offsets[:, first // 16 : last // 16]
-            nc.vector.tensor_copy(out=picked_words[:, first:last], in_=all_words[:, 0:reach].indirect(entries))
-            nc.vector.tensor_copy(out=picked_bytes[:, first:last], in_=all_bytes[:, 0:reach].indirect(entries))
+            nc.vector.tensor_copy(out=picked[:, first:last], in_=window[:, 0:reach].indirect(entries))
 
         h_grouped = []
         h_codes = []
@@ -137,77 +147,84 @@ def tile_picked_pick_glu_silu_srt_e_kernel(tc, xT, w1, w3, w2, offs, out):
                 in_=h_grouped[g][:, first:last, :].rearrange("p n t -> p (n t)"),
             )
 
-        def output(first, last, engines):
-            width = last - first
-            per_bank = 512 // width
-            m = 0
-            for number, engine in enumerate(engines):
-                bank = acc.tile([P, per_bank, width], F32, name="y%d_%d" % (first, number), tag="gate" if number % 2 == 0 else "up")
-                for i in range(per_bank):
-                    rows = slice((m + i) * P, (m + i + 1) * P)
-                    for g in range(2):
-                        nc.tensor.matmul_mx(
-                            out=bank[:, i, :],
-                            lhsT=codes["w2_%d" % g][:, rows].bitcast(FP8X4),
-                            lhsT_scale=scales["w2_%d" % g][:, rows],
-                            rhs=h_codes[g][:, first:last].bitcast(FP8X4),
-                            rhs_scale=h_scales[g][:, first:last],
-                            start=(g == 0),
-                            stop=(g == 1),
-                        )
-                y = keep.tile([P, per_bank, width], F32, name="y_out%d_%d" % (first, number))
-                if engine == "S":
-                    nc.scalar.copy(y[:], bank[:])
-                else:
-                    nc.vector.tensor_copy(out=y[:], in_=bank[:])
-                nc.sync.dma_start(
-                    out=out[m * P : (m + per_bank) * P, first:last].rearrange("(i p) n -> p i n", p=P), in_=y[:]
-                )
-                m = m + per_bank
+        y_banks = {}
 
-        cast("x0", (("V", 32), ("S", 96)))
+        def product(first, last, g):
+            for m in range(4):
+                rows = slice(m * P, (m + 1) * P)
+                if g == 0:
+                    bank = acc.tile([P, last - first], F32, name="y%d_%d" % (first, m), tag="gate" if m % 2 == 0 else "up")
+                    y_banks[first, m] = bank
+                nc.tensor.matmul_mx(
+                    out=y_banks[first, m][:],
+                    lhsT=codes["w2_%d" % g][:, rows].bitcast(FP8X4),
+                    lhsT_scale=scales["w2_%d" % g][:, rows],
+                    rhs=h_codes[g][:, first:last].bitcast(FP8X4),
+                    rhs_scale=h_scales[g][:, first:last],
+                    start=(g == 0),
+                    stop=(g == 1),
+                )
+
+        def store(first, last, engines):
+            for m, engine in enumerate(engines):
+                y = keep.tile([P, last - first], F32, name="y_out%d_%d" % (first, m))
+                if engine == "S":
+                    nc.scalar.copy(y[:], y_banks[first, m][:])
+                else:
+                    nc.vector.tensor_copy(out=y[:], in_=y_banks[first, m][:])
+                nc.sync.dma_start(out=out[m * P : (m + 1) * P, first:last], in_=y[:])
+
+        cast("x0", (("S", 64), ("V", 64)))
         quantize("x0")
-        cast("x1", (("V", 32), ("S", 96)))
+        cast("x1", (("V", 48), ("S", 80)))
         quantize("x1")
-        cast("x2", (("V", 32), ("S", 96)))
+        cast("x2", (("V", 48), ("S", 80)))
         quantize("x2")
-        gather(0, 512)
-        cast("x3", (("V", 32), ("S", 96)))
+        gather(picked_words, all_words, 0, 512)
+        gather(picked_bytes, all_bytes, 0, 512)
+        cast("x3", (("V", 48), ("S", 80)))
         quantize("x3")
-        gather(512, 1024)
-        cast("w1_0", (("S", 128),))
+        cast("w1_0", (("V", 48), ("S", 80)))
         quantize("w1_0")
         cast("w3_0", (("V", 80), ("S", 48)))
         quantize("w3_0")
         unit(0, 0)
+        gather(picked_words, all_words, 512, 1024)
         unit(0, 1)
-        cast("w1_1", (("V", 16), ("S", 112)))
+        gather(picked_bytes, all_bytes, 512, 1024)
+        cast("w1_1", (("V", 32), ("S", 48), ("S", 48)))
         unit(0, 2)
         quantize("w1_1")
         unit(0, 3)
-        cast("w3_1", (("V", 16), ("S", 112)))
+        cast("w3_1", (("V", 32), ("S", 48), ("S", 48)))
         unit(0, 4)
         quantize_h(0, 0, 512)
         quantize("w3_1")
+        unit(0, 5)
         unit(1, 0)
+        cast("w2_0", (("G", 32), ("G", 32), ("G", 32), ("G", 32)))
         unit(1, 1)
-        cast("w2_0", (("V", 16), ("S", 112)))
         unit(1, 2)
         quantize("w2_0")
         unit(1, 3)
-        cast("w2_1", (("V", 16), ("S", 112)))
-        unit(0, 5)
-        quantize_h(1, 0, 512)
+        cast("w2_1", (("G", 32), ("G", 32), ("G", 32), ("G", 32)))
         unit(0, 6)
-        quantize("w2_1")
-        output(0, 512, "SVSV")
+        quantize_h(1, 0, 512)
         unit(0, 7)
+        quantize("w2_1")
+        product(0, 512, 0)
+        product(0, 512, 1)
         unit(1, 4)
         quantize_h(0, 512, 1024)
+        store(0, 512, "SVSS")
         unit(1, 5)
         unit(1, 6)
         quantize_h(1, 512, 768)
         unit(1, 7)
-        output(512, 768, "SV")
+        product(512, 768, 0)
+        product(512, 768, 1)
+        store(512, 768, "SVSV")
+        product(768, 1024, 0)
         quantize_h(1, 768, 1024)
-        output(768, 1024, "SV")
+        product(768, 1024, 1)
+        store(768, 1024, "SVSV")

@@ -44,33 +44,29 @@ def tile_picked_pick_glu_silu_srt_e_kernel(tc, xT, w1, w3, w2, offs, out):
             sources["w3_%d" % g] = w3[:, g * 512 : (g + 1) * 512]
             sources["w2_%d" % g] = w2[g * 512 : (g + 1) * 512, :]
         raw = {}
-        for name in ["x0","offs","x1","x2","x3","w1_0","w3_0","w1_1","w3_1","w2_0","w2_1"]:
+        for name in ["x0","x1","offs","x2","x3","w1_0","w3_0","w1_1","w3_1","w2_0","w2_1"]:
             if name == "offs":
                 nc.sync.dma_start(offsets[:], offs)
             else:
                 tile = keep.tile([P, PACK, 512], F32, name="raw_" + name, align_bytes=64)
-                source = sources[name].rearrange("(p j) c -> p j c", j=PACK)
-                if name == "x0":
-                    for part in (slice(0, 256), slice(256, 512)):
-                        nc.sync.dma_start(out=tile[:, :, part], in_=source[:, :, part])
-                else:
-                    nc.sync.dma_start(out=tile[:], in_=source)
-                raw[name] = tile
+                nc.sync.dma_start(out=tile[:], in_=sources[name].rearrange("(p j) c -> p j c", j=PACK))
+                raw[name] = tile[:]
 
         grouped = {}
         codes = {}
         scales = {}
 
-        def cast(name, shares):
-            tile = keep.tile([P, 2048], BF16, name="grouped_" + name, align_bytes=64)
-            grouped[name] = tile
+        def cast(name, shares, start=0):
+            if start == 0:
+                fresh = keep.tile([P, 2048], BF16, name="grouped_" + name, align_bytes=64)
+                grouped[name] = fresh
+            tile = grouped[name]
             if name[:2] in ("w1", "w3"):
                 dst = tile[:].rearrange("p (t m j) -> p m j t", t=PACK, j=PACK)
-                src = raw[name][:].rearrange("p j (m t) -> p m j t", t=PACK)
+                src = raw[name].rearrange("p j (m t) -> p m j t", t=PACK)
             else:
                 dst = tile[:].rearrange("p (c i j) -> p c j i", i=4, j=PACK)
-                src = raw[name][:].rearrange("p j (c i) -> p c j i", i=4)
-            start = 0
+                src = raw[name].rearrange("p j (c i) -> p c j i", i=4)
             for engine, count in shares:
                 part = slice(start, start + count)
                 if engine == "V":
@@ -78,17 +74,17 @@ def tile_picked_pick_glu_silu_srt_e_kernel(tc, xT, w1, w3, w2, offs, out):
                 elif engine == "S":
                     nc.scalar.activation(dst[:, part], src[:, part], COPY)
                 else:
-                    cols = slice(start * 4, (start + count) * 4)
+                    if name[:2] == "w2":
+                        cols = slice(start * 4, (start + count) * 4)
+                        flat_dst = tile[:].rearrange("p (c j) -> p c j", j=PACK)[:, cols]
+                        flat_src = raw[name].rearrange("p j c -> p c j")[:, cols]
+                    else:
+                        flat_dst = tile[:].rearrange("p (t m j) -> p t m j", t=PACK, j=PACK)[:, :, part]
+                        flat_src = raw[name].rearrange("p j (m t) -> p t m j", t=PACK)[:, :, part]
                     nc.gpsimd.tensor_scalar(
-                        out=tile[:].rearrange("p (c j) -> p c j", j=PACK)[:, cols],
-                        in0=raw[name][:].rearrange("p j c -> p c j")[:, cols],
-                        scalar1=1.0,
-                        scalar2=0.0,
-                        op0=MULT,
-                        op1=mybir.AluOpType.add,
+                        out=flat_dst, in0=flat_src, scalar1=1.0, scalar2=0.0, op0=MULT, op1=mybir.AluOpType.add
                     )
                 start = start + count
-            assert start == 128
 
         def quantize(name):
             if name[0] == "x":
@@ -174,33 +170,38 @@ def tile_picked_pick_glu_silu_srt_e_kernel(tc, xT, w1, w3, w2, offs, out):
                     nc.vector.tensor_copy(out=y[:], in_=y_banks[first, m][:])
                 nc.sync.dma_start(out=out[m * P : (m + 1) * P, first:last], in_=y[:])
 
-        cast("x0", (("S", 64), ("V", 64)))
+        cast("x0", (("V", 64), ("S", 64)))
         quantize("x0")
-        cast("x1", (("V", 48), ("S", 80)))
+        cast("x1", (("V", 44), ("S", 84)))
         quantize("x1")
-        cast("x2", (("V", 48), ("S", 80)))
+        cast("x2", (("V", 44), ("S", 84)))
         quantize("x2")
         gather(picked_words, all_words, 0, 512)
         gather(picked_bytes, all_bytes, 0, 512)
-        cast("x3", (("V", 48), ("S", 80)))
+        cast("x3", (("V", 32), ("S", 96)))
         quantize("x3")
-        cast("w1_0", (("V", 48), ("S", 80)))
+        cast("w1_0", (("S", 128),))
         quantize("w1_0")
-        cast("w3_0", (("V", 80), ("S", 48)))
+        gather(picked_words, all_words, 512, 1024)
+        cast("w3_0", (("V", 64), ("S", 64)))
         quantize("w3_0")
         unit(0, 0)
-        gather(picked_words, all_words, 512, 1024)
         unit(0, 1)
         gather(picked_bytes, all_bytes, 512, 1024)
-        cast("w1_1", (("V", 32), ("S", 48), ("S", 48)))
+        cast("w1_1", (("V", 24), ("S", 36)))
+        cast("w1_1", (("S", 34),), 60)
         unit(0, 2)
-        quantize("w1_1")
+        cast("w1_1", (("S", 34),), 94)
         unit(0, 3)
-        cast("w3_1", (("V", 32), ("S", 48), ("S", 48)))
+        quantize("w1_1")
+        cast("w3_1", (("V", 24), ("S", 36)))
         unit(0, 4)
         quantize_h(0, 0, 512)
-        quantize("w3_1")
+        cast("w3_1", (("S", 34),), 60)
         unit(0, 5)
+        cast("w3_1", (("S", 34),), 94)
+        unit(0, 6)
+        quantize("w3_1")
         unit(1, 0)
         cast("w2_0", (("G", 32), ("G", 32), ("G", 32), ("G", 32)))
         unit(1, 1)
@@ -208,16 +209,15 @@ def tile_picked_pick_glu_silu_srt_e_kernel(tc, xT, w1, w3, w2, offs, out):
         quantize("w2_0")
         unit(1, 3)
         cast("w2_1", (("G", 32), ("G", 32), ("G", 32), ("G", 32)))
-        unit(0, 6)
-        quantize_h(1, 0, 512)
         unit(0, 7)
+        quantize_h(1, 0, 512)
+        unit(1, 4)
         quantize("w2_1")
+        quantize_h(0, 512, 1024)
         product(0, 512, 0)
         product(0, 512, 1)
-        unit(1, 4)
-        quantize_h(0, 512, 1024)
-        store(0, 512, "SVSS")
         unit(1, 5)
+        store(0, 512, "SVSV")
         unit(1, 6)
         quantize_h(1, 512, 768)
         unit(1, 7)

from contextlib import ExitStack

import concourse.mybir as mybir

K, T, S, H, N = 512, 2048, 1024, 1024, 512

F32 = mybir.dt.float32
BF16 = mybir.dt.bfloat16
U32 = mybir.dt.uint32
U16 = mybir.dt.uint16
U8 = mybir.dt.uint8
FP8X4 = mybir.dt.float8_e4m3fn_x4
COPY = mybir.ActivationFunctionType.Copy
SILU = mybir.ActivationFunctionType.Silu
MULT = mybir.AluOpType.mult

P = 128
PACK = 4
PASS = P * PACK
SLICE = 128
FLOPS = 2 * S * (2 * K * H + H * N)


def tile_picked_pick_glu_silu_srt_e_kernel(tc, xT, w1, w3, w2, offs, out):
    nc = tc.nc
    with ExitStack() as ctx:
        keep = ctx.enter_context(tc.tile_pool(name="keep", bufs=1))
        ring = ctx.enter_context(tc.tile_pool(name="ring", bufs=4))
        acc = ctx.enter_context(tc.psum_pool(name="acc", bufs=4))

        offsets = keep.tile([P, S // 16], U16, name="offsets")
        warm = keep.tile([P, 1], F32, name="warm")
        nc.vector.memset(warm[:], 0.0)
        nc.scalar.activation(warm[:], warm[:], SILU)
        all_bytes = keep.tile([P, T], U8, name="all_bytes", align_bytes=64)
        nc.gpsimd.memset(all_bytes[:], 0)
        all_words = keep.tile([P, T], U32, name="all_words", align_bytes=64)

        sources = {}
        for c in range(4):
            sources["x%d" % c] = xT[:, c * 512 : (c + 1) * 512]
        for g in range(2):
            sources["w1_%d" % g] = w1[:, g * 512 : (g + 1) * 512]
            sources["w3_%d" % g] = w3[:, g * 512 : (g + 1) * 512]
            sources["w2_%d" % g] = w2[g * 512 : (g + 1) * 512, :]
        raw = {}
        for name in ["x0","x1","offs","x2","x3","w1_0","w3_0","w1_1","w3_1","w2_0","w2_1"]:
            if name == "offs":
                nc.sync.dma_start(offsets[:], offs)
            else:
                tile = keep.tile([P, PACK, 512], F32, name="raw_" + name, align_bytes=64)
                nc.sync.dma_start(out=tile[:], in_=sources[name].rearrange("(p j) c -> p j c", j=PACK))
                raw[name] = tile[:]

        grouped = {}
        codes = {}
        scales = {}

        def cast(name, shares, start=0):
            if start == 0:
                fresh = keep.tile([P, 2048], BF16, name="grouped_" + name, align_bytes=64)
                grouped[name] = fresh
            tile = grouped[name]
            if name[:2] in ("w1", "w3"):
                dst = tile[:].rearrange("p (t m j) -> p m j t", t=PACK, j=PACK)
                src = raw[name].rearrange("p j (m t) -> p m j t", t=PACK)
            else:
                dst = tile[:].rearrange("p (c i j) -> p c j i", i=4, j=PACK)
                src = raw[name].rearrange("p j (c i) -> p c j i", i=4)
            for engine, count in shares:
                part = slice(start, start + count)
                if engine == "V":
                    nc.vector.tensor_copy(out=dst[:, part], in_=src[:, part])
                elif engine == "S":
                    nc.scalar.activation(dst[:, part], src[:, part], COPY)
                else:
                    if name[:2] == "w2":
                        cols = slice(start * 4, (start + count) * 4)
                        flat_dst = tile[:].rearrange("p (c j) -> p c j", j=PACK)[:, cols]
                        flat_src = raw[name].rearrange("p j c -> p c j")[:, cols]
                    else:
                        flat_dst = tile[:].rearrange("p (t m j) -> p t m j", t=PACK, j=PACK)[:, :, part]
                        flat_src = raw[name].rearrange("p j (m t) -> p t m j", t=PACK)[:, :, part]
                    nc.gpsimd.tensor_scalar(
                        out=flat_dst, in0=flat_src, scalar1=1.0, scalar2=0.0, op0=MULT, op1=mybir.AluOpType.add
                    )
                start = start + count

        def quantize(name):
            if name[0] == "x":
                cols = slice(int(name[1:]) * 512, (int(name[1:]) + 1) * 512)
                nc.vector.quantize_mx(out=all_words[:, cols].bitcast(FP8X4), scales=all_bytes[:, cols], in_=grouped[name][:])
            else:
                code = keep.tile([P, 512], U32, name="codes_" + name, align_bytes=64)
                scale = keep.tile([P, 512], U8, name="scales_" + name, align_bytes=64)
                nc.vector.quantize_mx(out=code[:].bitcast(FP8X4), scales=scale[:], in_=grouped[name][:])
                codes[name] = code
                scales[name] = scale

        picked_words = keep.tile([P, S], U32, name="picked_words", align_bytes=64)
        picked_bytes = keep.tile([P, S], U8, name="picked_bytes", align_bytes=64)

        def gather(picked, window, first, last):
            reach = last + T - S
            entries = offsets[:, first // 16 : last // 16]
            nc.vector.tensor_copy(out=picked[:, first:last], in_=window[:, 0:reach].indirect(entries))

        h_grouped = []
        h_codes = []
        h_scales = []
        for g in range(2):
            a = keep.tile([P, S, PACK], BF16, name="h_grouped%d" % g, align_bytes=64)
            b = keep.tile([P, S], U32, name="h_codes%d" % g, align_bytes=64)
            c = keep.tile([P, S], U8, name="h_scales%d" % g, align_bytes=64)
            h_grouped.append(a)
            h_codes.append(b)
            h_scales.append(c)

        def unit(g, s):
            cols = slice(s * SLICE, (s + 1) * SLICE)
            gate = acc.tile([P, PACK, SLICE], F32, name="gate", tag="gate")
            up = acc.tile([P, PACK, SLICE], F32, name="up", tag="up")
            for layer, bank in (("w1_%d", gate), ("w3_%d", up)):
                for t in range(PACK):
                    rows = slice(t * P, (t + 1) * P)
                    nc.tensor.matmul_mx(
                        out=bank[:, t, :],
                        lhsT=codes[layer % g][:, rows].bitcast(FP8X4),
                        lhsT_scale=scales[layer % g][:, rows],
                        rhs=picked_words[:, cols].bitcast(FP8X4),
                        rhs_scale=picked_bytes[:, cols],
                        start=True,
                        stop=True,
                    )
            act = ring.tile([P, SLICE, PACK], F32, name="act")
            nc.scalar.activation(act[:], gate[:].rearrange("p t n -> p n t"), SILU)
            nc.vector.tensor_tensor(out=h_grouped[g][:, cols, :], in0=up[:].rearrange("p t n -> p n t"), in1=act[:], op=MULT)

        def quantize_h(g, first, last):
            nc.vector.quantize_mx(
                out=h_codes[g][:, first:last].bitcast(FP8X4),
                scales=h_scales[g][:, first:last],
                in_=h_grouped[g][:, first:last, :].rearrange("p n t -> p (n t)"),
            )

        y_banks = {}

        def product(first, last, g):
            for m in range(4):
                rows = slice(m * P, (m + 1) * P)
                if g == 0:
                    bank = acc.tile([P, last - first], F32, name="y%d_%d" % (first, m), tag="gate" if m % 2 == 0 else "up")
                    y_banks[first, m] = bank
                nc.tensor.matmul_mx(
                    out=y_banks[first, m][:],
                    lhsT=codes["w2_%d" % g][:, rows].bitcast(FP8X4),
                    lhsT_scale=scales["w2_%d" % g][:, rows],
                    rhs=h_codes[g][:, first:last].bitcast(FP8X4),
                    rhs_scale=h_scales[g][:, first:last],
                    start=(g == 0),
                    stop=(g == 1),
                )

        def store(first, last, engines):
            for m, engine in enumerate(engines):
                y = keep.tile([P, last - first], F32, name="y_out%d_%d" % (first, m))
                if engine == "S":
                    nc.scalar.copy(y[:], y_banks[first, m][:])
                else:
                    nc.vector.tensor_copy(out=y[:], in_=y_banks[first, m][:])
                nc.sync.dma_start(out=out[m * P : (m + 1) * P, first:last], in_=y[:])

        cast("x0", (("V", 64), ("S", 64)))
        quantize("x0")
        cast("x1", (("V", 44), ("S", 84)))
        quantize("x1")
        cast("x2", (("V", 44), ("S", 84)))
        quantize("x2")
        gather(picked_words, all_words, 0, 512)
        gather(picked_bytes, all_bytes, 0, 512)
        cast("x3", (("V", 32), ("S", 96)))
        quantize("x3")
        cast("w1_0", (("S", 128),))
        quantize("w1_0")
        gather(picked_words, all_words, 512, 1024)
        cast("w3_0", (("V", 64), ("S", 64)))
        quantize("w3_0")
        unit(0, 0)
        unit(0, 1)
        gather(picked_bytes, all_bytes, 512, 1024)
        cast("w1_1", (("V", 24), ("S", 36)))
        cast("w1_1", (("S", 34),), 60)
        unit(0, 2)
        cast("w1_1", (("S", 34),), 94)
        unit(0, 3)
        quantize("w1_1")
        cast("w3_1", (("V", 24), ("S", 36)))
        unit(0, 4)
        quantize_h(0, 0, 512)
        cast("w3_1", (("S", 34),), 60)
        unit(0, 5)
        cast("w3_1", (("S", 34),), 94)
        unit(0, 6)
        quantize("w3_1")
        unit(1, 0)
        cast("w2_0", (("G", 32), ("G", 32), ("G", 32), ("G", 32)))
        unit(1, 1)
        unit(1, 2)
        quantize("w2_0")
        unit(1, 3)
        cast("w2_1", (("G", 32), ("G", 32), ("G", 32), ("G", 32)))
        unit(0, 7)
        quantize_h(1, 0, 512)
        unit(1, 4)
        quantize("w2_1")
        quantize_h(0, 512, 1024)
        product(0, 512, 0)
        product(0, 512, 1)
        unit(1, 5)
        store(0, 512, "SVSV")
        unit(1, 6)
        quantize_h(1, 512, 768)
        unit(1, 7)
        product(512, 768, 0)
        product(512, 768, 1)
        store(512, 768, "SVSV")
        product(768, 1024, 0)
        quantize_h(1, 768, 1024)
        product(768, 1024, 1)
        store(768, 1024, "SVSV")
